import numpy as np, ml_dtypes
CORES = [10,11,138,139,266,267,394,395]
N = 8
T = 8
ROUTE = [[[5,2,7],[1,2,7],[7,3,6],[2,7,0],[3,6,0],[2,6,7],[5,0,1],[1,5,3]],[[6,5,2],[1,6,4],[5,4,2],[4,0,2],[0,5,4],[0,7,6],[7,2,0],[1,0,3]],[[5,2,4],[3,6,1],[1,2,4],[5,4,0],[6,0,7],[7,2,5],[4,2,1],[6,0,3]],[[4,0,2],[4,0,5],[5,2,0],[6,2,3],[4,1,0],[2,0,1],[4,0,6],[1,7,4]],[[6,4,1],[0,2,6],[7,5,3],[7,4,5],[5,1,4],[4,0,7],[5,0,7],[5,2,1]],[[3,6,2],[5,2,3],[6,3,1],[7,4,1],[2,1,5],[5,1,7],[0,7,6],[6,0,4]],[[6,0,7],[6,3,0],[5,4,6],[7,1,5],[0,3,5],[6,5,2],[7,6,0],[2,7,6]],[[1,5,3],[4,7,1],[6,5,7],[2,5,7],[5,7,2],[0,6,3],[2,1,5],[4,5,3]]]
ZW = 29
def setup_inputs(rng):
    return {"z": rng.standard_normal((N, 128, ZW), dtype=np.float32).astype(ml_dtypes.bfloat16)}
def reference(z):
    y = np.zeros((N, 128, T), np.float64)
    fill = [0] * N
    for r in range(N):
        for t in range(T):
            for e in ROUTE[r][t]:
                y[r][:, t] += z[e][:, fill[e]].astype(np.float64)
                fill[e] += 1
    return {"y": y.astype(z.dtype)}

@@ -1,0 +1,108 @@
+from concourse.bass import DstId, RemoteDMATransfer
+
+SCRATCH = {
+    "zs": ("sbuf", [128, 29], "bfloat16"),
+    "land": ("sbuf", [128, 48], "bfloat16"),
+    "rel": ("sbuf", [128, 32], "bfloat16"),
+    "res": ("sbuf", [128, 8], "bfloat16"),
+}
+SEMAPHORES = ["loaded", "sent", "a1", "a2", "done", "stored"]
+
+H = 4
+
+
+def helper(h):
+    return h * 128 + 8
+
+
+def plan(tables):
+    route = tables["ROUTE"]
+    n = len(route)
+    held = [[] for _ in range(n)]
+    for r in range(n):
+        for t in range(len(route[r])):
+            for e in route[r][t]:
+                held[e].append((r, t))
+    blk = [[None] * H for _ in range(n)]
+    for e in range(n):
+        for h in range(H):
+            idx = [k for k, (r, t) in enumerate(held[e]) if r // 2 == h]
+            blk[e][h] = (idx[0] if idx else 0, len(idx))
+    loff = [[0] * n for _ in range(H)]
+    for h in range(H):
+        a = 0
+        for e in range(n):
+            loff[h][e] = a
+            a += blk[e][h][1]
+    return route, held, blk, loff
+
+
+def rank_program(g, core, T, topo):
+    route, held, blk, loff = plan(T.tables)
+    rank = T.rank_of(core)
+    h = topo.host(core)
+    if rank is not None:
+        g.dma_start(T.zs[:], T.z[:]).then_inc(T.sem.loaded, 16)
+        g.wait_ge(T.sem.loaded, 16)
+        sent = 0
+        for dh in (2, 1, 3, 0):
+            hd = (h + dh) % H
+            a, w = blk[rank][hd]
+            if w == 0:
+                continue
+            if dh == 2:
+                x = helper((h + 1) % H)
+                o = 0 if rank % 2 == 0 else blk[rank - 1][hd][1]
+                out = T.rel[:, o:o + w]
+            else:
+                x = helper(hd)
+                o = loff[hd][rank]
+                out = T.land[:, o:o + w]
+            rid, pid = topo.addr(x, core)
+            m = topo.mask(core, x)
+            g.remote_dma(out, T.zs[:, a:a + w], T.sem.a1, T.sem.sent, pid, rid, m)
+            sent += bin(m).count("1")
+        g.wait_ge(T.sem.sent, sent)
+        g.wait_ge(T.sem.done, len(route[rank]))
+        g.dma_start(T.y[:], T.res[:]).then_inc(T.sem.stored, 16)
+        g.wait_ge(T.sem.stored, 16)
+        return
+    if core != helper(h):
+        return
+    n1 = 0
+    for e in range(len(route)):
+        dh = (h - e // 2) % H
+        if dh == 0 and blk[e][h][1]:
+            n1 += 16
+        if dh in (1, 3) and blk[e][h][1]:
+            n1 += 8
+        if dh == 1 and blk[e][(h + 1) % H][1]:
+            n1 += 8
+    g.wait_ge(T.sem.a1, n1)
+    sent = 0
+    hs, hd = (h - 1) % H, (h + 1) % H
+    w = blk[2 * hs][hd][1] + blk[2 * hs + 1][hd][1]
+    if w:
+        x = helper(hd)
+        rid, pid = topo.addr(x, core)
+        o = loff[hd][2 * hs]
+        g.remote_dma(T.land[:, o:o + w], T.rel[:, 0:w], T.sem.a2, T.sem.sent, pid, rid, 0xFF)
+        sent += 8
+    hs = (h + 2) % H
+    if blk[2 * hs][h][1] + blk[2 * hs + 1][h][1]:
+        g.wait_ge(T.sem.a2, 8)
+    trs = []
+    k = 0
+    for r in (2 * h, 2 * h + 1):
+        rid, pid = topo.addr(T.cores[r], core)
+        for t in range(len(route[r])):
+            srcs = []
+            for e in route[r][t]:
+                c = loff[h][e] + held[e].index((r, t)) - blk[e][h][0]
+                srcs.append(T.land[:, c:c + 1])
+            trs.append(RemoteDMATransfer(dst_ids=[DstId(rid=rid, pnc=pid)], dma_engine_mask=1 << k,
+                                         remote_sem=T.sem.done, srcs=srcs, dsts=[T.res[:, t:t + 1]], alu_op=1))
+            k += 1
+    g.remote_dma_fused(trs, local_sem=T.sem.sent)
+    sent += k
+    g.wait_ge(T.sem.sent, sent)

@@ -1,108 +1,139 @@
 from concourse.bass import DstId, RemoteDMATransfer
+from concourse.mybir import AluOpType
 
 SCRATCH = {
     "zs": ("sbuf", [128, 29], "bfloat16"),
-    "land": ("sbuf", [128, 48], "bfloat16"),
-    "rel": ("sbuf", [128, 32], "bfloat16"),
-    "res": ("sbuf", [128, 8], "bfloat16"),
+    "land": ("sbuf", [128, 24], "bfloat16"),
+    "resA": ("sbuf", [128, 8], "bfloat16"),
+    "resB": ("sbuf", [128, 8], "bfloat16"),
 }
-SEMAPHORES = ["loaded", "sent", "a1", "a2", "done", "stored"]
+SEMAPHORES = ["loaded", "sent", "arrived", "gotA", "gotB", "stored", "added"]
 
-H = 4
-
-
-def helper(h):
-    return h * 128 + 8
+A_CORE = (0, 4)
+B_CORE = (1, 5)
 
 
-def plan(tables):
-    route = tables["ROUTE"]
+def bits(m):
+    return bin(m).count("1")
+
+
+def helper_core(role, h, b):
+    return h * 128 + 8 + (A_CORE if role == "A" else B_CORE)[b]
+
+
+def blocks(route):
     n = len(route)
-    held = [[] for _ in range(n)]
+    blk = [[None] * n for _ in range(n)]
+    fill = [0] * n
     for r in range(n):
-        for t in range(len(route[r])):
-            for e in route[r][t]:
-                held[e].append((r, t))
-    blk = [[None] * H for _ in range(n)]
-    for e in range(n):
-        for h in range(H):
-            idx = [k for k, (r, t) in enumerate(held[e]) if r // 2 == h]
-            blk[e][h] = (idx[0] if idx else 0, len(idx))
-    loff = [[0] * n for _ in range(H)]
-    for h in range(H):
-        a = 0
         for e in range(n):
-            loff[h][e] = a
-            a += blk[e][h][1]
-    return route, held, blk, loff
+            blk[e][r] = (fill[e], [t for t in range(len(route[r])) if e in route[r][t]])
+            fill[e] += len(blk[e][r][1])
+    return blk
+
+
+def split_engines(n, avail):
+    cnt = [1] * n
+    grown = True
+    while grown:
+        grown = False
+        for i in range(n):
+            if sum(cnt) + cnt[i] <= avail:
+                cnt[i] *= 2
+                grown = True
+    masks, at = [], 0
+    for c in cnt:
+        masks.append(((1 << c) - 1) << at)
+        at += c
+    return masks
+
+
+def job(route, blk, role, h, b):
+    rd = 2 * (3 - h) + b if role == "A" else 2 * h + b
+    experts = [e for e in range(len(route)) if e // 2 in (h, h ^ 1)]
+    off, a = {}, 0
+    for e in experts:
+        off[e] = a
+        a += len(blk[e][rd][1])
+    other = "B" if role == "A" else "A"
+    todo = []
+    for t in range(len(route[rd])):
+        cols = [off[e] + blk[e][rd][1].index(t) for e in route[rd][t] if e in experts]
+        if not cols:
+            continue
+        if len(cols) == len(route[rd][t]) and len(cols) > 1:
+            todo.append((cols[:-1], role, t))
+            todo.append((cols[-1:], other, t))
+        else:
+            todo.append((cols, role, t))
+    avail = 8 if role == "A" else 16
+    calls = []
+    for k in range(0, len(todo), avail):
+        part = todo[k:k + avail]
+        calls.append([p + (m,) for p, m in zip(part, split_engines(len(part), avail))])
+    return rd, experts, off, calls
 
 
 def rank_program(g, core, T, topo):
-    route, held, blk, loff = plan(T.tables)
-    rank = T.rank_of(core)
+    route = T.tables["ROUTE"]
+    blk = blocks(route)
     h = topo.host(core)
+    rank = T.rank_of(core)
+
     if rank is not None:
-        g.dma_start(T.zs[:], T.z[:]).then_inc(T.sem.loaded, 16)
+        g.sync.dma_start(T.zs[:], T.z[:]).then_inc(T.sem.loaded, 16)
         g.wait_ge(T.sem.loaded, 16)
-        sent = 0
-        for dh in (2, 1, 3, 0):
-            hd = (h + dh) % H
-            a, w = blk[rank][hd]
-            if w == 0:
-                continue
-            if dh == 2:
-                x = helper((h + 1) % H)
-                o = 0 if rank % 2 == 0 else blk[rank - 1][hd][1]
-                out = T.rel[:, o:o + w]
+        order = []
+        for r in range(len(route)):
+            hr = r // 2
+            if topo.rack(hr) == topo.rack(h):
+                role, hx = "B", hr
             else:
-                x = helper(hd)
-                o = loff[hd][rank]
-                out = T.land[:, o:o + w]
+                role, hx = "A", 3 - hr
+            order.append(((role == "B") * 2 + (hx == h), r, role, hx))
+        sent = 0
+        for _, r, role, hx in sorted(order):
+            a, toks = blk[rank][r]
+            if not toks:
+                continue
+            x = helper_core(role, hx, r % 2)
+            o = job(route, blk, role, hx, r % 2)[2][rank]
             rid, pid = topo.addr(x, core)
             m = topo.mask(core, x)
-            g.remote_dma(out, T.zs[:, a:a + w], T.sem.a1, T.sem.sent, pid, rid, m)
-            sent += bin(m).count("1")
+            g.remote_dma(T.land[:, o:o + len(toks)], T.zs[:, a:a + len(toks)], T.sem.arrived, T.sem.sent, pid, rid, m)
+            sent += bits(m)
+        got = {"A": 0, "B": 0}
+        for role, hx in (("A", 3 - h), ("B", h)):
+            for call in job(route, blk, role, hx, rank % 2)[3]:
+                for _, row, _, m in call:
+                    got[row] += bits(m)
+        g.sync.wait_ge(T.sem.gotB, got["B"])
+        g.sync.dma_start(T.y[:], T.resB[:]).then_inc(T.sem.stored, 16)
         g.wait_ge(T.sem.sent, sent)
-        g.wait_ge(T.sem.done, len(route[rank]))
-        g.dma_start(T.y[:], T.res[:]).then_inc(T.sem.stored, 16)
+        g.wait_ge(T.sem.gotA, got["A"])
         g.wait_ge(T.sem.stored, 16)
+        g.dma_start(T.y[:], T.resA[:], accum_op=AluOpType.add).then_inc(T.sem.added, 16)
+        g.wait_ge(T.sem.added, 16)
         return
-    if core != helper(h):
-        return
-    n1 = 0
-    for e in range(len(route)):
-        dh = (h - e // 2) % H
-        if dh == 0 and blk[e][h][1]:
-            n1 += 16
-        if dh in (1, 3) and blk[e][h][1]:
-            n1 += 8
-        if dh == 1 and blk[e][(h + 1) % H][1]:
-            n1 += 8
-    g.wait_ge(T.sem.a1, n1)
-    sent = 0
-    hs, hd = (h - 1) % H, (h + 1) % H
-    w = blk[2 * hs][hd][1] + blk[2 * hs + 1][hd][1]
-    if w:
-        x = helper(hd)
-        rid, pid = topo.addr(x, core)
-        o = loff[hd][2 * hs]
-        g.remote_dma(T.land[:, o:o + w], T.rel[:, 0:w], T.sem.a2, T.sem.sent, pid, rid, 0xFF)
-        sent += 8
-    hs = (h + 2) % H
-    if blk[2 * hs][h][1] + blk[2 * hs + 1][h][1]:
-        g.wait_ge(T.sem.a2, 8)
-    trs = []
-    k = 0
-    for r in (2 * h, 2 * h + 1):
-        rid, pid = topo.addr(T.cores[r], core)
-        for t in range(len(route[r])):
-            srcs = []
-            for e in route[r][t]:
-                c = loff[h][e] + held[e].index((r, t)) - blk[e][h][0]
-                srcs.append(T.land[:, c:c + 1])
-            trs.append(RemoteDMATransfer(dst_ids=[DstId(rid=rid, pnc=pid)], dma_engine_mask=1 << k,
-                                         remote_sem=T.sem.done, srcs=srcs, dsts=[T.res[:, t:t + 1]], alu_op=1))
-            k += 1
-    g.remote_dma_fused(trs, local_sem=T.sem.sent)
-    sent += k
-    g.wait_ge(T.sem.sent, sent)
+
+    for role in ("A", "B"):
+        for b in (0, 1):
+            if core != helper_core(role, h, b):
+                continue
+            rd, experts, off, calls = job(route, blk, role, h, b)
+            dst = T.cores[rd]
+            rid, pid = topo.addr(dst, core)
+            n = sum(bits(topo.mask(T.cores[e], core)) for e in experts if blk[e][rd][1])
+            g.wait_ge(T.sem.arrived, n)
+            sent = 0
+            for call in calls:
+                trs = []
+                for cols, row, t, m in call:
+                    out = (T.resA if row == "A" else T.resB)[:, t:t + 1]
+                    sem = T.sem.gotA if row == "A" else T.sem.gotB
+                    trs.append(RemoteDMATransfer(dst_ids=[DstId(rid=rid, pnc=pid)], dma_engine_mask=m, remote_sem=sem,
+                                                 srcs=[T.land[:, c:c + 1] for c in cols], dsts=[out],
+                                                 alu_op=1 if len(cols) > 1 else 0))
+                    sent += bits(m)
+                g.remote_dma_fused(trs, local_sem=T.sem.sent)
+            g.wait_ge(T.sem.sent, sent)

@@ -21,6 +21,10 @@ def helper_core(role, h, b):
     return h * 128 + 8 + (A_CORE if role == "A" else B_CORE)[b]
 
 
+def send_mask(topo, src, dst):
+    return 0x00FF if topo.mask(src, dst) == 0x00FF else 0xFF00
+
+
 def blocks(route):
     n = len(route)
     blk = [[None] * n for _ in range(n)]
@@ -81,7 +85,8 @@ def rank_program(g, core, T, topo):
     rank = T.rank_of(core)
 
     if rank is not None:
-        g.sync.dma_start(T.zs[:], T.z[:]).then_inc(T.sem.loaded, 16)
+        held = sum(len(blk[rank][r][1]) for r in range(len(route)))
+        g.sync.dma_start(T.zs[:, 0:held], T.z[:, 0:held]).then_inc(T.sem.loaded, 16)
         g.wait_ge(T.sem.loaded, 16)
         order = []
         for r in range(len(route)):
@@ -99,7 +104,7 @@ def rank_program(g, core, T, topo):
             x = helper_core(role, hx, r % 2)
             o = job(route, blk, role, hx, r % 2)[2][rank]
             rid, pid = topo.addr(x, core)
-            m = topo.mask(core, x)
+            m = send_mask(topo, core, x)
             g.remote_dma(T.land[:, o:o + len(toks)], T.zs[:, a:a + len(toks)], T.sem.arrived, T.sem.sent, pid, rid, m)
             sent += bits(m)
         got = {"A": 0, "B": 0}
@@ -123,7 +128,7 @@ def rank_program(g, core, T, topo):
             rd, experts, off, calls = job(route, blk, role, h, b)
             dst = T.cores[rd]
             rid, pid = topo.addr(dst, core)
-            n = sum(bits(topo.mask(T.cores[e], core)) for e in experts if blk[e][rd][1])
+            n = sum(bits(send_mask(topo, T.cores[e], core)) for e in experts if blk[e][rd][1])
             g.wait_ge(T.sem.arrived, n)
             sent = 0
             for call in calls:

from concourse.bass import DstId, RemoteDMATransfer
from concourse.mybir import AluOpType

SCRATCH = {
    "zs": ("sbuf", [128, 29], "bfloat16"),
    "land": ("sbuf", [128, 24], "bfloat16"),
    "resA": ("sbuf", [128, 8], "bfloat16"),
    "resB": ("sbuf", [128, 8], "bfloat16"),
}
SEMAPHORES = ["loaded", "sent", "arrived", "gotA", "gotB", "stored", "added"]

A_CORE = (0, 4)
B_CORE = (1, 5)


def bits(m):
    return bin(m).count("1")


def helper_core(role, h, b):
    return h * 128 + 8 + (A_CORE if role == "A" else B_CORE)[b]


def send_mask(topo, src, dst):
    return 0x00FF if topo.mask(src, dst) == 0x00FF else 0xFF00


def blocks(route):
    n = len(route)
    blk = [[None] * n for _ in range(n)]
    fill = [0] * n
    for r in range(n):
        for e in range(n):
            blk[e][r] = (fill[e], [t for t in range(len(route[r])) if e in route[r][t]])
            fill[e] += len(blk[e][r][1])
    return blk


def split_engines(n, avail):
    cnt = [1] * n
    grown = True
    while grown:
        grown = False
        for i in range(n):
            if sum(cnt) + cnt[i] <= avail:
                cnt[i] *= 2
                grown = True
    masks, at = [], 0
    for c in cnt:
        masks.append(((1 << c) - 1) << at)
        at += c
    return masks


def job(route, blk, role, h, b):
    rd = 2 * (3 - h) + b if role == "A" else 2 * h + b
    experts = [e for e in range(len(route)) if e // 2 in (h, h ^ 1)]
    off, a = {}, 0
    for e in experts:
        off[e] = a
        a += len(blk[e][rd][1])
    other = "B" if role == "A" else "A"
    todo = []
    for t in range(len(route[rd])):
        cols = [off[e] + blk[e][rd][1].index(t) for e in route[rd][t] if e in experts]
        if not cols:
            continue
        if len(cols) == len(route[rd][t]) and len(cols) > 1:
            todo.append((cols[:-1], role, t))
            todo.append((cols[-1:], other, t))
        else:
            todo.append((cols, role, t))
    avail = 8 if role == "A" else 16
    calls = []
    for k in range(0, len(todo), avail):
        part = todo[k:k + avail]
        calls.append([p + (m,) for p, m in zip(part, split_engines(len(part), avail))])
    return rd, experts, off, calls


def rank_program(g, core, T, topo):
    route = T.tables["ROUTE"]
    blk = blocks(route)
    h = topo.host(core)
    rank = T.rank_of(core)

    if rank is not None:
        held = sum(len(blk[rank][r][1]) for r in range(len(route)))
        g.sync.dma_start(T.zs[:, 0:held], T.z[:, 0:held]).then_inc(T.sem.loaded, 16)
        g.wait_ge(T.sem.loaded, 16)
        order = []
        for r in range(len(route)):
            hr = r // 2
            if topo.rack(hr) == topo.rack(h):
                role, hx = "B", hr
            else:
                role, hx = "A", 3 - hr
            order.append(((role == "B") * 2 + (hx == h), r, role, hx))
        sent = 0
        for _, r, role, hx in sorted(order):
            a, toks = blk[rank][r]
            if not toks:
                continue
            x = helper_core(role, hx, r % 2)
            o = job(route, blk, role, hx, r % 2)[2][rank]
            rid, pid = topo.addr(x, core)
            m = send_mask(topo, core, x)
            g.remote_dma(T.land[:, o:o + len(toks)], T.zs[:, a:a + len(toks)], T.sem.arrived, T.sem.sent, pid, rid, m)
            sent += bits(m)
        got = {"A": 0, "B": 0}
        for role, hx in (("A", 3 - h), ("B", h)):
            for call in job(route, blk, role, hx, rank % 2)[3]:
                for _, row, _, m in call:
                    got[row] += bits(m)
        g.sync.wait_ge(T.sem.gotB, got["B"])
        g.sync.dma_start(T.y[:], T.resB[:]).then_inc(T.sem.stored, 16)
        g.wait_ge(T.sem.sent, sent)
        g.wait_ge(T.sem.gotA, got["A"])
        g.wait_ge(T.sem.stored, 16)
        g.dma_start(T.y[:], T.resA[:], accum_op=AluOpType.add).then_inc(T.sem.added, 16)
        g.wait_ge(T.sem.added, 16)
        return

    for role in ("A", "B"):
        for b in (0, 1):
            if core != helper_core(role, h, b):
                continue
            rd, experts, off, calls = job(route, blk, role, h, b)
            dst = T.cores[rd]
            rid, pid = topo.addr(dst, core)
            n = sum(bits(send_mask(topo, T.cores[e], core)) for e in experts if blk[e][rd][1])
            g.wait_ge(T.sem.arrived, n)
            sent = 0
            for call in calls:
                trs = []
                for cols, row, t, m in call:
                    out = (T.resA if row == "A" else T.resB)[:, t:t + 1]
                    sem = T.sem.gotA if row == "A" else T.sem.gotB
                    trs.append(RemoteDMATransfer(dst_ids=[DstId(rid=rid, pnc=pid)], dma_engine_mask=m, remote_sem=sem,
                                                 srcs=[T.land[:, c:c + 1] for c in cols], dsts=[out],
                                                 alu_op=1 if len(cols) > 1 else 0))
                    sent += bits(m)
                g.remote_dma_fused(trs, local_sem=T.sem.sent)
            g.wait_ge(T.sem.sent, sent)
